import numpy as np
import ml_dtypes


def mxq(x, axis, fmt="e4m3"):
    dtype, down = {"e4m3": (ml_dtypes.float8_e4m3fn, 7), "e5m2": (ml_dtypes.float8_e5m2, 14)}[fmt]
    v = np.moveaxis(np.asarray(x, np.float32).astype(ml_dtypes.bfloat16).astype(np.float64), axis, -1)
    blocks = v.reshape(v.shape[:-1] + (-1, 32))
    amax = np.abs(blocks).max(-1, keepdims=True)
    byte = np.maximum(np.where(amax > 0, np.frexp(amax)[1] - 1 + 127, 0) - down, 1)
    scale = np.exp2(byte - 127.0)
    codes = (blocks / scale).astype(np.float32).astype(dtype).astype(np.float64)
    return np.moveaxis((codes * scale).reshape(v.shape), -1, axis)


WIDE = False


def mx_kscale(k):
    if not WIDE:
        return np.ones(k)
    levels = np.array([24, -24, 12, -12, 0])
    if k % 512:
        return np.exp2(np.random.permutation(np.resize(levels, k // 32))).repeat(32)
    a = np.empty((k // 512, 16))
    for p in range(k // 512):
        a[p, :8] = np.random.permutation(np.resize(levels, 8))
        for g in range(8):
            far = levels[np.abs(levels - a[p, g]) >= 10]
            a[p, g + 8] = far[np.random.randint(len(far))]
    return np.exp2(a.ravel()).repeat(32)


def f64(x):
    return np.asarray(x).astype(np.float64)


E2M1 = np.array([0.0, 0.5, 1.0, 1.5, 2.0, 3.0, 4.0, 6.0, -0.0, -0.5, -1.0, -1.5, -2.0, -3.0, -4.0, -6.0])


def pack_weight(w, fmt):
    k, n = w.shape
    w = f64(np.asarray(w, np.float32).astype(ml_dtypes.bfloat16)).reshape(k // 32, 32, n)
    amax = np.abs(w).max(1)
    if fmt == "e4m3":
        byte = np.frexp(amax)[1] - 1 + 127 - 7
    else:
        mant, ex = np.frexp(amax / 6.0)
        byte = np.where(mant > 0.5, ex, ex - 1) + 127
    byte = np.clip(np.where(amax > 0, byte, 1), 1, 254)
    scaled = (w * np.exp2(127.0 - byte)[:, None, :]).reshape(k, n).astype(np.float32)
    by_word = np.ascontiguousarray(scaled.reshape(k // 512, 128, 4, n).transpose(0, 1, 3, 2))
    if fmt == "e4m3":
        words = by_word.astype(ml_dtypes.float8_e4m3fn).view(np.uint8)
    else:
        c = by_word.astype(ml_dtypes.float4_e2m1fn).view(np.uint8) & 0xF
        words = (c[..., 0::2] | (c[..., 1::2] << 4)).reshape(k // 512, 128, 2 * n)
    return np.ascontiguousarray(words), np.ascontiguousarray(byte.astype(np.uint8).reshape(k // 512, 16, n))


def unpack_weight(words, scales, fmt):
    g, _, n = scales.shape
    words = np.ascontiguousarray(words).reshape(g, 128, n, -1)
    if fmt == "e4m3":
        vals = words.view(ml_dtypes.float8_e4m3fn).astype(np.float64)
    else:
        nib = np.empty((g, 128, n, 4), np.uint8)
        nib[..., 0::2] = words & 0xF
        nib[..., 1::2] = words >> 4
        vals = E2M1[nib]
    vals = vals * np.repeat(np.exp2(scales.astype(np.float64) - 127.0), 8, axis=1)[..., None]
    return vals.transpose(0, 1, 3, 2).reshape(g * 512, n)


K, N, T = 512, 512, 1024


def setup_inputs():
    n = np.random.standard_normal
    s = mx_kscale(K)[:, None]
    p_wr = pack_weight(n((K, N)) / np.sqrt(4 * K) / s, "e2m1")
    p_wi = pack_weight(n((K, N)) / np.sqrt(4 * K) / s, "e4m3")
    p_wj = pack_weight(n((K, N)) / np.sqrt(4 * K) / s, "e4m3")
    p_wk = pack_weight(n((K, N)) / np.sqrt(4 * K) / s, "e4m3")
    return {
        "xr": (n((K, T)) * s).astype(np.float32),
        "xi": (n((K, T)) * s).astype(np.float32),
        "xj": (n((K, T)) * s).astype(np.float32),
        "xk": (n((K, T)) * s).astype(np.float32),
        "wr_words": p_wr[0],
        "wr_scales": p_wr[1],
        "wi_words": p_wi[0],
        "wi_scales": p_wi[1],
        "wj_words": p_wj[0],
        "wj_scales": p_wj[1],
        "wk_words": p_wk[0],
        "wk_scales": p_wk[1],
    }


def reference(xr, xi, xj, xk, wr_words, wr_scales, wi_words, wi_scales, wj_words, wj_scales, wk_words, wk_scales):
    xr_ = mxq(f64(xr), 0, "e4m3")
    xi_ = mxq(f64(xi), 0, "e4m3")
    xj_ = mxq(f64(xj), 0, "e4m3")
    xk_ = mxq(f64(xk), 0, "e4m3")
    wr_ = unpack_weight(wr_words, wr_scales, "e2m1")
    wi_ = unpack_weight(wi_words, wi_scales, "e4m3")
    wj_ = unpack_weight(wj_words, wj_scales, "e4m3")
    wk_ = unpack_weight(wk_words, wk_scales, "e4m3")
    pr = wr_.T @ xr_
    mr = wi_.T @ xi_ + wj_.T @ xj_ + wk_.T @ xk_
    pi = wr_.T @ xi_ + wi_.T @ xr_ + wj_.T @ xk_
    mi = wk_.T @ xj_
    pj = wr_.T @ xj_ + wj_.T @ xr_ + wk_.T @ xi_
    mj = wi_.T @ xk_
    pk = wr_.T @ xk_ + wi_.T @ xj_ + wk_.T @ xr_
    mk = wj_.T @ xi_
    return (pr - mr) ** 2 + (pi - mi) ** 2 + (pj - mj) ** 2 + (pk - mk) ** 2

from contextlib import ExitStack

import concourse.mybir as mybir

K, N, T = 512, 512, 1024
FLOPS = 16 * 2 * K * N * T

F32 = mybir.dt.float32
BF16 = mybir.dt.bfloat16
U32 = mybir.dt.uint32
I32 = mybir.dt.int32
U8 = mybir.dt.uint8
FP8X4 = mybir.dt.float8_e4m3fn_x4
FP4X4 = mybir.dt.float4_e2m1fn_x4
ALU = mybir.AluOpType
ACT = mybir.ActivationFunctionType

P = 128
PACK = 4
BANK = 512
R, I, J, KK = 0, 1, 2, 3
LONE = [(R, R), (KK, J), (I, KK), (J, I)]
THREE = [
    [(I, I), (J, J), (KK, KK)],
    [(I, R), (R, I), (J, KK)],
    [(J, R), (R, J), (KK, I)],
    [(I, J), (KK, R), (R, KK)],
]
CHUNKS = [128, 128, 256, 256, 256]
HEAD_W = [I, J, KK, R]
G_PLANES = [R]
W_AFTER = {I: 0, J: 1, KK: 2, R: 2}
PLANE_AFTER = {I: 0, J: 1, KK: 3, R: 3}
Q_STEP = [1, 3, 5, 7, 11, 15, 19, 23]
IL_STEP = [0, 0, 1, 2, 3, 4, 5, 6, 8, 9, 12, 13, 16, 17, 20, 21]
IL_S = [1, 3, 5, 7, 9, 13]
S_COPY = list(range(32))
SQ_STEP = [g + 1 for g in range(32)]
G_STEP = {}
PAIR_STEP = {u: 4 * u + 7 for u in range(7)}
FINAL_STEP = {u: 4 * u + 8 for u in range(7)}
CHAIN_FROM = 7
GROUP_BUFS = 4


def tile_mix_quat_norm_kernel(
    tc, xr, xi, xj, xk, wr_words, wr_scales, wi_words, wi_scales, wj_words, wj_scales, wk_words, wk_scales, out
):
    nc = tc.nc
    xs = [xr, xi, xj, xk]
    w_words = [wr_words, wi_words, wj_words, wk_words]
    w_scales = [wr_scales, wi_scales, wj_scales, wk_scales]
    starts = [sum(CHUNKS[:c]) for c in range(len(CHUNKS))]

    with ExitStack() as ctx:
        keep = ctx.enter_context(tc.tile_pool(name="keep", bufs=1))
        stage = ctx.enter_context(tc.tile_pool(name="stage", bufs=4))
        psum = ctx.enter_context(tc.psum_pool(name="psum", bufs=1))
        ctx.enter_context(tc.manual_schedule(engines={mybir.EngineType.SP, mybir.EngineType.Pool}))

        w_codes, w_planes = {}, {}
        for a in G_PLANES + [a for a in HEAD_W if a not in G_PLANES]:
            w_planes[a] = keep.tile([P, N], U8, name="w_plane%d" % a, align_bytes=64)
            nc.vector.memset(w_planes[a][:].bitcast(I32), 0)

        def load_w(a):
            width = 2 * N if a == R else 4 * N
            w_codes[a] = keep.tile([P, width], U8, name="w_codes%d" % a, align_bytes=64)
            src = w_words[a][0] if a == R else w_words[a][0].rearrange("p n t -> p (n t)")
            nc.sync.dma_start(out=w_codes[a][:].bitcast(I32), in_=src.bitcast(I32))

        def load_plane(a, q):
            queue = nc.gpsimd if a in G_PLANES else nc.sync
            queue.dma_start(
                out=w_planes[a][32 * q : 32 * q + 4, :].bitcast(I32),
                in_=w_scales[a][0][4 * q : 4 * q + 4, :].bitcast(I32),
            )

        raw, codes, planes, grouped = {}, {}, {}, {}

        def load_x(c, b):
            width = CHUNKS[c]
            raw[c, b] = keep.tile([P, PACK, width], F32, name="raw%d_%d" % (c, b))
            src = xs[b][:, starts[c] : starts[c] + width].rearrange("(p j) t -> p j t", j=PACK)
            nc.sync.dma_start(out=raw[c, b][:], in_=src)

        for a in G_PLANES:
            for q in range(4):
                load_plane(a, q)
        for b in range(4):
            load_x(0, b)
            for a in HEAD_W:
                if W_AFTER[a] == b:
                    load_w(a)
            for a in HEAD_W:
                if PLANE_AFTER[a] == b and a not in G_PLANES:
                    for q in range(4):
                        load_plane(a, q)
        for c in range(1, len(CHUNKS)):
            for b in range(4):
                load_x(c, b)

        def share(c):
            return 1 if CHUNKS[c] == BANK else 2

        def interleave(c, n, on_scalar):
            width = min(CHUNKS[c], BANK // 2)
            h, half = divmod(n, 2)
            if half == 0:
                grouped[c, h] = keep.tile([P, 2 * BANK], F32, name="grouped", bufs=GROUP_BUFS, align_bytes=64)
            first = half * PACK * width
            dst = grouped[c, h][:].bitcast(BF16)[:, first : first + PACK * width]
            dst = dst.rearrange("p (c i j) -> p c j i", i=4, j=PACK)
            src = raw[c, n][:] if share(c) == 2 else raw[c, h][:, :, half * width : (half + 1) * width]
            src = src.rearrange("p j (c i) -> p c j i", i=4)
            if on_scalar:
                nc.scalar.activation(out=dst, in_=src, func=ACT.Copy)
            else:
                nc.vector.tensor_copy(out=dst, in_=src)

        def quantise(c, h, lo=0, hi=2):
            width = min(CHUNKS[c], BANK // 2)
            if lo == 0:
                codes[c, h] = keep.tile([P, 2 * width], U32, name="codes%d_%d" % (c, h), align_bytes=64)
                planes[c, h] = keep.tile([P, 2 * width], U8, name="plane%d_%d" % (c, h), align_bytes=64)
            nc.vector.quantize_mx(
                out=codes[c, h][:, lo * width : hi * width].bitcast(FP8X4),
                scales=planes[c, h][:, lo * width : hi * width],
                in_=grouped[c, h][:].bitcast(BF16)[:, lo * PACK * width : hi * PACK * width],
            )

        units = []
        for c in range(len(CHUNKS)):
            tiles = BANK // CHUNKS[c]
            for n0 in range(0, N // P, tiles):
                units.append((c, n0, tiles))
        steps = 4 * len(units)

        def passes_of(u, bank, a, b, lone):
            c, n0, tiles = units[u]
            width = CHUNKS[c]
            cut = P if (a == R and width == 256 and not lone) else width
            made = []
            for h in range(tiles):
                for t0 in range(0, width, cut):
                    made.append((bank[:, h * width + t0 : h * width + t0 + cut], a, n0 + h, c, b, t0, cut))
            return made

        def matmul(dst, a, nt, c, b, t0, cut, start, stop):
            if a == R:
                lhsT = w_codes[a][:, 2 * P * nt : 2 * P * (nt + 1)].bitcast(FP4X4)
            else:
                lhsT = w_codes[a][:, 4 * P * nt : 4 * P * (nt + 1)].bitcast(FP8X4)
            first = (b % share(c)) * CHUNKS[c] + t0
            nc.tensor.matmul_mx(
                out=dst,
                lhsT=lhsT,
                lhsT_scale=w_planes[a][:, P * nt : P * (nt + 1)],
                rhs=codes[c, b // share(c)][:, first : first + cut].bitcast(FP8X4),
                rhs_scale=planes[c, b // share(c)][:, first : first + cut],
                start=start,
                stop=stop,
            )

        pairs_of = {}
        lone_bank, three_bank, lone_sb, diff, sq, acc = {}, {}, {}, {}, {}, {}

        def mm_lone(g):
            u, part = divmod(g, 4)
            lone_bank[g] = psum.tile([P, BANK], F32, name="lone_bank%d" % part)
            for made in passes_of(u, lone_bank[g], *LONE[part], True):
                matmul(*made, True, True)

        def mm_three(g, which, first, last):
            u, part = divmod(g, 4)
            if first:
                three_bank[g] = psum.tile([P, BANK], F32, name="three_bank%d" % part)
            made = passes_of(u, three_bank[g], *THREE[part][which], False)
            for n in range(len(made)):
                matmul(*made[n], first and n == 0, last and n == len(made) - 1)

        def copy_lone(g):
            lone_sb[g] = stage.tile([P, BANK], F32, name="lone_sb")
            if g in S_COPY:
                nc.scalar.copy(out=lone_sb[g][:], in_=lone_bank[g][:])
            else:
                nc.vector.tensor_copy(out=lone_sb[g][:], in_=lone_bank[g][:])

        def subtract(g):
            diff[g] = stage.tile([P, BANK], F32, name="diff", bufs=10)
            if g % 4 == R:
                nc.vector.tensor_tensor(out=diff[g][:], in0=lone_sb[g][:], in1=three_bank[g][:], op=ALU.subtract)
            else:
                nc.vector.tensor_tensor(out=diff[g][:], in0=three_bank[g][:], in1=lone_sb[g][:], op=ALU.subtract)

        def square(g):
            u, part = divmod(g, 4)
            if part == 0:
                sq[u] = stage.tile([P, 4 * BANK], F32, name="sq", bufs=6)
            nc.scalar.activation(out=sq[u][:, part * BANK : (part + 1) * BANK], in_=diff[g][:], func=ACT.Square)

        def store(u, src):
            c, n0, tiles = units[u]
            dst = out.rearrange("(h p) t -> p h t", p=P)[:, n0 : n0 + tiles, starts[c] : starts[c] + CHUNKS[c]]
            nc.sync.dma_start(out=dst, in_=src[:].rearrange("p (h t) -> p h t", h=tiles))

        def add_on_gpsimd(u, pairs):
            nc.gpsimd.tensor_tensor(out=pairs[:], in0=sq[u][:, : 2 * BANK], in1=sq[u][:, 2 * BANK :], op=ALU.add)
            total = stage.tile([P, BANK], F32, name="acc", bufs=8)
            nc.gpsimd.tensor_tensor(out=total[:], in0=pairs[:, :BANK], in1=pairs[:, BANK:], op=ALU.add)
            store(u, total)

        def add_pairs(u):
            pairs_of[u] = stage.tile([P, 2 * BANK], F32, name="pairs", bufs=2)
            nc.vector.tensor_tensor(out=pairs_of[u][:], in0=sq[u][:, : 2 * BANK], in1=sq[u][:, 2 * BANK :], op=ALU.add)

        def add_final(u):
            total = stage.tile([P, BANK], F32, name="acc", bufs=8)
            nc.vector.tensor_tensor(out=total[:], in0=pairs_of[u][:, :BANK], in1=pairs_of[u][:, BANK:], op=ALU.add)
            store(u, total)

        def add_on_vector(g):
            u, part = divmod(g, 4)
            acc[g] = stage.tile([P, BANK], F32, name="acc", bufs=8)
            before = sq[u][:, :BANK] if part == 1 else acc[g - 1][:]
            nc.vector.tensor_tensor(out=acc[g][:], in0=before, in1=sq[u][:, part * BANK : (part + 1) * BANK], op=ALU.add)
            if part == 3:
                store(u, acc[g])

        for b in range(4):
            interleave(0, b, False)
            quantise(0, b // 2, b % 2, b % 2 + 1)
        mm_lone(0)
        later = [(c, h) for c in range(1, len(CHUNKS)) for h in range(4 // share(c))]
        copy_lone(0)
        for g in range(steps + 20):
            if g in Q_STEP:
                quantise(*later[Q_STEP.index(g)])
            if g in G_STEP:
                add_on_gpsimd(G_STEP[g], grouped[later[Q_STEP.index(g)]])
            if g + 1 < steps:
                mm_lone(g + 1)
            if g < steps:
                for w in range(3):
                    mm_three(g, w, w == 0, w == 2)
            if g + 1 < steps:
                copy_lone(g + 1)
            if g < steps:
                subtract(g)
            for n in range(steps):
                if SQ_STEP[n] == g:
                    square(n)
            for n in range(len(IL_STEP)):
                if IL_STEP[n] == g:
                    interleave(later[n // 2][0], 2 * later[n // 2][1] + n % 2, n in IL_S)
            for u in range(len(units)):
                if FINAL_STEP.get(u) == g:
                    add_final(u)
                if PAIR_STEP.get(u) == g:
                    add_pairs(u)
            if g - 2 > 4 * CHAIN_FROM and g - 2 < steps:
                add_on_vector(g - 2)
